import numpy as np
import ml_dtypes


def mxq(x, axis, fmt="e4m3"):
    dtype, down = {"e4m3": (ml_dtypes.float8_e4m3fn, 7), "e5m2": (ml_dtypes.float8_e5m2, 14)}[fmt]
    v = np.moveaxis(np.asarray(x, np.float32).astype(ml_dtypes.bfloat16).astype(np.float64), axis, -1)
    blocks = v.reshape(v.shape[:-1] + (-1, 32))
    amax = np.abs(blocks).max(-1, keepdims=True)
    byte = np.maximum(np.where(amax > 0, np.frexp(amax)[1] - 1 + 127, 0) - down, 1)
    scale = np.exp2(byte - 127.0)
    codes = (blocks / scale).astype(np.float32).astype(dtype).astype(np.float64)
    return np.moveaxis((codes * scale).reshape(v.shape), -1, axis)


WIDE = False


def mx_kscale(k):
    if not WIDE:
        return np.ones(k)
    levels = np.array([10, -10, 5, -5, 0])
    if k % 512:
        return np.exp2(np.random.permutation(np.resize(levels, k // 32))).repeat(32)
    a = np.empty((k // 512, 16))
    for p in range(k // 512):
        a[p, :8] = np.random.permutation(np.resize(levels, 8))
        for g in range(8):
            far = levels[np.abs(levels - a[p, g]) >= 10]
            a[p, g + 8] = far[np.random.randint(len(far))]
    return np.exp2(a.ravel()).repeat(32)


def f64(x):
    return np.asarray(x).astype(np.float64)


def striped(idx):
    return np.tile(np.asarray(idx).reshape(-1, 16).T, (8, 1)).astype(np.uint16)


def unstriped(offs):
    return offs[:16].T.reshape(-1).astype(np.int64)


E2M1 = np.array([0.0, 0.5, 1.0, 1.5, 2.0, 3.0, 4.0, 6.0, -0.0, -0.5, -1.0, -1.5, -2.0, -3.0, -4.0, -6.0])


def pack_weight(w, fmt):
    k, n = w.shape
    w = f64(np.asarray(w, np.float32).astype(ml_dtypes.bfloat16)).reshape(k // 32, 32, n)
    amax = np.abs(w).max(1)
    if fmt == "e4m3":
        byte = np.frexp(amax)[1] - 1 + 127 - 7
    else:
        mant, ex = np.frexp(amax / 6.0)
        byte = np.where(mant > 0.5, ex, ex - 1) + 127
    byte = np.clip(np.where(amax > 0, byte, 1), 1, 254)
    scaled = (w * np.exp2(127.0 - byte)[:, None, :]).reshape(k, n).astype(np.float32)
    by_word = np.ascontiguousarray(scaled.reshape(k // 512, 128, 4, n).transpose(0, 1, 3, 2))
    if fmt == "e4m3":
        words = by_word.astype(ml_dtypes.float8_e4m3fn).view(np.uint8)
    else:
        c = by_word.astype(ml_dtypes.float4_e2m1fn).view(np.uint8) & 0xF
        words = (c[..., 0::2] | (c[..., 1::2] << 4)).reshape(k // 512, 128, 2 * n)
    return np.ascontiguousarray(words), np.ascontiguousarray(byte.astype(np.uint8).reshape(k // 512, 16, n))


def unpack_weight(words, scales, fmt):
    g, _, n = scales.shape
    words = np.ascontiguousarray(words).reshape(g, 128, n, -1)
    if fmt == "e4m3":
        vals = words.view(ml_dtypes.float8_e4m3fn).astype(np.float64)
    else:
        nib = np.empty((g, 128, n, 4), np.uint8)
        nib[..., 0::2] = words & 0xF
        nib[..., 1::2] = words >> 4
        vals = E2M1[nib]
    vals = vals * np.repeat(np.exp2(scales.astype(np.float64) - 127.0), 8, axis=1)[..., None]
    return vals.transpose(0, 1, 3, 2).reshape(g * 512, n)


D, T, I, J, U, E = 512, 2048, 512, 512, 1024, 512


def setup_inputs():
    n = np.random.standard_normal
    idx = np.random.permutation(T)[:I]
    idx2 = np.random.permutation(U)[:J]
    idx3 = np.random.permutation(U)[:J]
    idx4 = np.random.permutation(U)[:J]
    fd = mx_kscale(D)
    fi = mx_kscale(I)
    ti = np.ones(T)
    ti[idx] = fi
    keysp = pack_weight(n((D, T)) / fd[:, None], "e4m3")
    return {
        "keys_words": keysp[0],
        "keys_scales": keysp[1],
        "notes": (n((D, U)) * 1.0 / np.sqrt(D) * fd[:, None]).astype(np.float32),
        "rowf": (np.random.uniform(0.02, 0.08, (I, 1)) * fi[:, None]).astype(np.float32),
        "vals": (n((E, T)) / ti).astype(np.float32),
        "offs": striped(idx),
        "offs2": striped(idx2),
        "offs3": striped(idx3),
        "offs4": striped(idx4),
    }


def reference(keys_words, keys_scales, notes, rowf, vals, offs, offs2, offs3, offs4):
    idx = unstriped(offs)
    idx2 = unstriped(offs2)
    idx3 = unstriped(offs3)
    idx4 = unstriped(offs4)
    keysu = unpack_weight(keys_words, keys_scales, "e4m3")
    keysidxg = keysu[:, idx]
    notesq = mxq(f64(notes), 0, "e4m3")
    g1 = keysidxg.T @ notesq
    lo2 = np.minimum(g1[:, idx2], g1[:, idx3])
    hi2 = np.maximum(g1[:, idx2], g1[:, idx3])
    g0 = np.maximum(lo2, np.minimum(hi2, g1[:, idx4]))
    gr1 = g0 * f64(rowf)
    vt1 = f64(vals)[:, idx].T
    vt1q = mxq(vt1, 0, "e4m3")
    gr1q = mxq(gr1, 0, "e4m3")
    o = vt1q.T @ gr1q
    return o

@@ -1,0 +1,205 @@
+from contextlib import ExitStack
+
+import concourse.mybir as mybir
+from concourse.masks import make_identity
+
+D, T, I, J, U, E = 512, 2048, 512, 512, 1024, 512
+FLOPS = 2 * D * I * U + 2 * I * E * J
+
+F32 = mybir.dt.float32
+BF16 = mybir.dt.bfloat16
+I32 = mybir.dt.int32
+U32 = mybir.dt.uint32
+U16 = mybir.dt.uint16
+U8 = mybir.dt.uint8
+FP8X4 = mybir.dt.float8_e4m3fn_x4
+ALU = mybir.AluOpType
+COPY = mybir.ActivationFunctionType.Copy
+
+P = 128
+PACK = 4
+NOTE_CHUNK = 256
+J_CHUNK = 256
+BANK = 512
+
+
+def tile_attend_tab_middleof3_exchange_kernel(tc, keys_words, keys_scales, notes, rowf, vals, offs, offs2, offs3, offs4, out):
+    nc = tc.nc
+    with ExitStack() as ctx:
+        keep = ctx.enter_context(tc.tile_pool(name="keep", bufs=1))
+        acc_pool = ctx.enter_context(tc.psum_pool(name="acc", bufs=6))
+        turn_pool = ctx.enter_context(tc.psum_pool(name="turn", bufs=2))
+
+        token_list = keep.tile([P, I // 16], U16, name="token_list")
+        nc.sync.dma_start(token_list[:], offs)
+
+        key_scale_pool = keep.tile([P, T], U8, name="key_scale_pool", align_bytes=64)
+        nc.vector.memset(key_scale_pool[:].bitcast(I32), 0)
+        note_rows = notes.rearrange("(p t) u -> p t u", t=PACK)
+        note_raw = [keep.tile([P, PACK, NOTE_CHUNK], F32, name="note_raw%d" % c) for c in range(U // NOTE_CHUNK)]
+
+        def load_notes(c):
+            nc.sync.dma_start(out=note_raw[c][:], in_=note_rows[:, :, c * NOTE_CHUNK : (c + 1) * NOTE_CHUNK])
+
+        load_notes(0)
+        for q in range(4):
+            nc.sync.dma_start(
+                out=key_scale_pool[32 * q : 32 * q + 4, :].bitcast(I32),
+                in_=keys_scales[0, 4 * q : 4 * q + 4, :].bitcast(I32),
+            )
+        key_word_pool = keep.tile([P, T], I32, name="key_word_pool", align_bytes=64)
+        nc.sync.dma_start(out=key_word_pool[:], in_=keys_words[0].rearrange("p n t -> p (n t)").bitcast(I32))
+        for c in range(1, U // NOTE_CHUNK):
+            load_notes(c)
+
+        column_lists = []
+        for n, src in enumerate((offs2, offs3, offs4)):
+            lst = keep.tile([P, J // 16], U16, name="column_list%d" % n)
+            nc.sync.dma_start(lst[:], src)
+            column_lists.append(lst)
+        row_factor = keep.tile([P, PACK], F32, name="row_factor")
+        nc.sync.dma_start(out=row_factor[:], in_=rowf.rearrange("(p t) o -> p (t o)", t=PACK))
+
+        val_pool = []
+        for k in range(E // P):
+            vp = keep.tile([P, T], F32, name="val_pool%d" % k)
+            nc.sync.dma_start(out=vp[:], in_=vals[k * P : (k + 1) * P, :])
+            val_pool.append(vp)
+
+        ident = keep.tile([P, P], F32, name="ident")
+        make_identity(nc, ident[:])
+
+        key_scales = keep.tile([P, I], U8, name="key_scales", align_bytes=64)
+        nc.vector.tensor_copy(
+            key_scales[:].rearrange("p (t s) -> p s t", t=PACK), key_scale_pool[:].indirect(token_list[:])
+        )
+        key_words = keep.tile([P, I], U32, name="key_words", align_bytes=64)
+        nc.vector.tensor_copy(
+            key_words[:].rearrange("p (t s) -> p s t", t=PACK),
+            key_word_pool[:].bitcast(U32).indirect(token_list[:]),
+        )
+
+        g1 = [keep.tile([P, U], F32, name="g1_%d" % t) for t in range(PACK)]
+        for c in range(U // NOTE_CHUNK):
+            grouped = keep.tile([P, NOTE_CHUNK, PACK], BF16, name="note_grouped%d" % c, align_bytes=64)
+            nc.vector.tensor_copy(
+                out=grouped[:].rearrange("p (c i) t -> p c t i", i=4),
+                in_=note_raw[c][:].rearrange("p t (c i) -> p c t i", i=4),
+            )
+            codes = keep.tile([P, NOTE_CHUNK], U32, name="note_codes%d" % c, align_bytes=64)
+            scales = keep.tile([P, NOTE_CHUNK], U8, name="note_scales%d" % c, align_bytes=64)
+            nc.vector.quantize_mx(
+                out=codes[:].bitcast(FP8X4), scales=scales[:], in_=grouped[:].rearrange("p u t -> p (u t)")
+            )
+            for t in range(PACK):
+                acc = acc_pool.tile([P, BANK], F32, name="acc")
+                nc.tensor.matmul_mx(
+                    out=acc[:, :NOTE_CHUNK],
+                    lhsT=key_words[:, t * P : (t + 1) * P].bitcast(FP8X4),
+                    lhsT_scale=key_scales[:, t * P : (t + 1) * P],
+                    rhs=codes[:].bitcast(FP8X4),
+                    rhs_scale=scales[:],
+                    start=True,
+                    stop=True,
+                )
+                if c == U // NOTE_CHUNK - 1 and t < 2:
+                    nc.vector.tensor_copy(out=g1[t][:, c * NOTE_CHUNK : (c + 1) * NOTE_CHUNK], in_=acc[:, :NOTE_CHUNK])
+                else:
+                    nc.scalar.copy(out=g1[t][:, c * NOTE_CHUNK : (c + 1) * NOTE_CHUNK], in_=acc[:, :NOTE_CHUNK])
+
+        def gather(on_vector, dst, window):
+            if on_vector:
+                nc.vector.tensor_copy(dst, window)
+            else:
+                nc.scalar.activation(dst, window, COPY)
+
+        chunks = J // J_CHUNK
+        picked = [[keep.tile([P, PACK, J_CHUNK], F32, name="picked%d_%d" % (h, n)) for n in range(3)] for h in range(chunks)]
+
+        def look_up(h, t, vector_lists):
+            cols = slice(h * J_CHUNK // 16, (h + 1) * J_CHUNK // 16)
+            for n in range(3):
+                gather(n in vector_lists, picked[h][n][:, t, :], g1[t][:].indirect(column_lists[n][:, cols]))
+
+        def middle(h, ts):
+            a, b, c = (picked[h][n] for n in range(3))
+            lo = keep.tile([P, PACK, J_CHUNK], F32, name="lo%d" % h)
+            for t0 in ts:
+                s = slice(t0, t0 + 2)
+                nc.vector.tensor_tensor(lo[:, s, :], a[:, s, :], b[:, s, :], ALU.min)
+                nc.vector.tensor_tensor(a[:, s, :], a[:, s, :], b[:, s, :], ALU.max)
+            for t0 in ts:
+                s = slice(t0, t0 + 2)
+                nc.vector.tensor_tensor(c[:, s, :], a[:, s, :], c[:, s, :], ALU.min)
+            for t0 in ts:
+                s = slice(t0, t0 + 2)
+                nc.vector.tensor_tensor(b[:, s, :], lo[:, s, :], c[:, s, :], ALU.max)
+            return b
+
+        def scale_and_quantise(h, g0):
+            grouped = keep.tile([P, J_CHUNK, PACK], BF16, name="table_grouped%d" % h, tag="grouped%d" % h, align_bytes=64)
+            nc.vector.tensor_tensor(
+                grouped[:].rearrange("p (c i) t -> p c t i", i=4),
+                g0[:].rearrange("p t (c i) -> p c t i", i=4),
+                row_factor[:].unsqueeze(1).unsqueeze(3).broadcast_to([P, J_CHUNK // 4, PACK, 4]),
+                ALU.mult,
+            )
+            codes = keep.tile([P, J_CHUNK], U32, name="table_codes%d" % h, align_bytes=64)
+            scales = keep.tile([P, J_CHUNK], U8, name="table_scales%d" % h, align_bytes=64)
+            nc.vector.quantize_mx(
+                out=codes[:].bitcast(FP8X4), scales=scales[:], in_=grouped[:].rearrange("p j t -> p (j t)")
+            )
+            return codes, scales
+
+        def turn_values():
+            grouped = keep.tile([P, E, PACK], BF16, name="val_grouped", tag="grouped1", align_bytes=64)
+            grouped_words = grouped[:].rearrange("p e t -> p (e t)").bitcast(F32).rearrange("p (k e u) -> p k e u", k=E // P, u=2)
+            for k0 in range(0, E // P, 2):
+                turned = turn_pool.tile([P, 2, 2, P], F32, name="turned")
+                for k in range(k0, k0 + 2):
+                    vp = keep.tile([P, I], BF16, name="val_picked%d" % k)
+                    nc.scalar.activation(vp[:], val_pool[k][:].indirect(token_list[:]), COPY)
+                    words = vp[:].bitcast(F32)
+                    for u in range(2):
+                        nc.tensor.transpose(turned[:, k - k0, u, :], words[:, u : I // 2 : 2], ident[:])
+                nc.scalar.copy(out=grouped_words[:, k0 : k0 + 2, :, :], in_=turned[:].rearrange("p k u e -> p k e u"))
+            codes = keep.tile([P, E], U32, name="val_codes", align_bytes=64)
+            scales = keep.tile([P, E], U8, name="val_scales", align_bytes=64)
+            return grouped, codes, scales
+
+        out_rows = out.rearrange("(k p) j -> p k j", p=P)
+
+        def second_product(h, val_codes, val_scales, codes, scales, engines):
+            for k0 in range(0, E // P, 2):
+                acc = acc_pool.tile([P, BANK], F32, name="acc")
+                for k in range(k0, k0 + 2):
+                    nc.tensor.matmul_mx(
+                        out=acc[:, (k - k0) * J_CHUNK : (k - k0 + 1) * J_CHUNK],
+                        lhsT=val_codes[:, k * P : (k + 1) * P].bitcast(FP8X4),
+                        lhsT_scale=val_scales[:, k * P : (k + 1) * P],
+                        rhs=codes[:].bitcast(FP8X4),
+                        rhs_scale=scales[:],
+                        start=True,
+                        stop=True,
+                    )
+                res = keep.tile([P, 2, J_CHUNK], F32, name="res%d_%d" % (h, k0))
+                if engines[k0 // 2]:
+                    nc.vector.tensor_copy(out=res[:].rearrange("p k j -> p (k j)"), in_=acc[:])
+                else:
+                    nc.scalar.copy(out=res[:].rearrange("p k j -> p (k j)"), in_=acc[:])
+                nc.sync.dma_start(out=out_rows[:, k0 : k0 + 2, h * J_CHUNK : (h + 1) * J_CHUNK], in_=res[:])
+
+        for t in range(PACK):
+            look_up(0, t, (0, 1) if t < 2 else (0,))
+        g0_first = middle(0, (0, 2))
+        for t in range(PACK):
+            look_up(1, t, (0,) if t < 3 else ())
+        table0 = scale_and_quantise(0, g0_first)
+        val_grouped, val_codes, val_scales = turn_values()
+        g0_second = middle(1, (0, 2))
+        nc.vector.quantize_mx(
+            out=val_codes[:].bitcast(FP8X4), scales=val_scales[:], in_=val_grouped[:].rearrange("p e t -> p (e t)")
+        )
+        second_product(0, val_codes, val_scales, table0[0], table0[1], (False, False))
+        table1 = scale_and_quantise(1, g0_second)
+        second_product(1, val_codes, val_scales, table1[0], table1[1], (True, False))

@@ -27,11 +27,16 @@ def tile_attend_tab_middleof3_exchange_kernel(tc, keys_words, keys_scales, notes
     nc = tc.nc
     with ExitStack() as ctx:
         keep = ctx.enter_context(tc.tile_pool(name="keep", bufs=1))
+        late = ctx.enter_context(tc.tile_pool(name="late", bufs=1))
         acc_pool = ctx.enter_context(tc.psum_pool(name="acc", bufs=6))
-        turn_pool = ctx.enter_context(tc.psum_pool(name="turn", bufs=2))
+        turn_pool = ctx.enter_context(tc.psum_pool(name="turn", bufs=1))
 
         token_list = keep.tile([P, I // 16], U16, name="token_list")
         nc.sync.dma_start(token_list[:], offs)
+        row_factor = keep.tile([P, PACK], F32, name="row_factor")
+        nc.sync.dma_start(out=row_factor[:], in_=rowf.rearrange("(p t) o -> p (t o)", t=PACK))
+        row_spread = keep.tile([P, PACK, J], F32, name="row_spread")
+        nc.scalar.copy(out=row_spread[:], in_=row_factor[:].unsqueeze(2).broadcast_to([P, PACK, J]))
 
         key_scale_pool = keep.tile([P, T], U8, name="key_scale_pool", align_bytes=64)
         nc.vector.memset(key_scale_pool[:].bitcast(I32), 0)
@@ -57,12 +62,10 @@ def tile_attend_tab_middleof3_exchange_kernel(tc, keys_words, keys_scales, notes
             lst = keep.tile([P, J // 16], U16, name="column_list%d" % n)
             nc.sync.dma_start(lst[:], src)
             column_lists.append(lst)
-        row_factor = keep.tile([P, PACK], F32, name="row_factor")
-        nc.sync.dma_start(out=row_factor[:], in_=rowf.rearrange("(p t) o -> p (t o)", t=PACK))
 
         val_pool = []
         for k in range(E // P):
-            vp = keep.tile([P, T], F32, name="val_pool%d" % k)
+            vp = keep.tile([P, T], F32, name="val_pool%d" % k, align_bytes=64)
             nc.sync.dma_start(out=vp[:], in_=vals[k * P : (k + 1) * P, :])
             val_pool.append(vp)
 
@@ -102,104 +105,119 @@ def tile_attend_tab_middleof3_exchange_kernel(tc, keys_words, keys_scales, notes
                     start=True,
                     stop=True,
                 )
-                if c == U // NOTE_CHUNK - 1 and t < 2:
+                if (c, t) in ((2, 3), (3, 0), (3, 1)):
                     nc.vector.tensor_copy(out=g1[t][:, c * NOTE_CHUNK : (c + 1) * NOTE_CHUNK], in_=acc[:, :NOTE_CHUNK])
                 else:
                     nc.scalar.copy(out=g1[t][:, c * NOTE_CHUNK : (c + 1) * NOTE_CHUNK], in_=acc[:, :NOTE_CHUNK])
 
-        def gather(on_vector, dst, window):
-            if on_vector:
-                nc.vector.tensor_copy(dst, window)
-            else:
-                nc.scalar.activation(dst, window, COPY)
+        a, b, c, lo, mid = (keep.tile([P, PACK, J], F32, name=n) for n in ("a", "b", "c", "lo", "mid"))
+        hi = late.tile([P, PACK, J], F32, name="hi", offset=4096, align_bytes=64)
 
-        chunks = J // J_CHUNK
-        picked = [[keep.tile([P, PACK, J_CHUNK], F32, name="picked%d_%d" % (h, n)) for n in range(3)] for h in range(chunks)]
+        def look_up_vector(t):
+            nc.vector.tensor_tensor(a[:, t, :], g1[t][:].indirect(column_lists[0][:]), row_spread[:, t, :], ALU.mult)
 
-        def look_up(h, t, vector_lists):
-            cols = slice(h * J_CHUNK // 16, (h + 1) * J_CHUNK // 16)
-            for n in range(3):
-                gather(n in vector_lists, picked[h][n][:, t, :], g1[t][:].indirect(column_lists[n][:, cols]))
+        def look_up_scalar(t):
+            nc.scalar.activation(b[:, t, :], g1[t][:].indirect(column_lists[1][:]), COPY)
+            if t < PACK - 1:
+                nc.scalar.activation(c[:, t, :], g1[t][:].indirect(column_lists[2][:]), COPY)
 
-        def middle(h, ts):
-            a, b, c = (picked[h][n] for n in range(3))
-            lo = keep.tile([P, PACK, J_CHUNK], F32, name="lo%d" % h)
-            for t0 in ts:
-                s = slice(t0, t0 + 2)
-                nc.vector.tensor_tensor(lo[:, s, :], a[:, s, :], b[:, s, :], ALU.min)
-                nc.vector.tensor_tensor(a[:, s, :], a[:, s, :], b[:, s, :], ALU.max)
-            for t0 in ts:
-                s = slice(t0, t0 + 2)
-                nc.vector.tensor_tensor(c[:, s, :], a[:, s, :], c[:, s, :], ALU.min)
-            for t0 in ts:
-                s = slice(t0, t0 + 2)
-                nc.vector.tensor_tensor(b[:, s, :], lo[:, s, :], c[:, s, :], ALU.max)
-            return b
+        def upper(t):
+            nc.vector.scalar_tensor_tensor(hi[:, t, :], b[:, t, :], row_factor[:, t : t + 1], a[:, t, :], ALU.mult, ALU.max)
 
-        def scale_and_quantise(h, g0):
-            grouped = keep.tile([P, J_CHUNK, PACK], BF16, name="table_grouped%d" % h, tag="grouped%d" % h, align_bytes=64)
+        def lower_and_cap(t):
+            nc.vector.scalar_tensor_tensor(lo[:, t, :], b[:, t, :], row_factor[:, t : t + 1], a[:, t, :], ALU.mult, ALU.min)
+            nc.vector.scalar_tensor_tensor(mid[:, t, :], c[:, t, :], row_factor[:, t : t + 1], hi[:, t, :], ALU.mult, ALU.min)
+
+        halves = J // J_CHUNK
+        table_grouped = [late.tile([P, J_CHUNK, PACK], BF16, name="table_grouped%d" % h, offset=1024 * h, align_bytes=64) for h in range(halves)]
+        table_codes = [keep.tile([P, J_CHUNK], U32, name="table_codes%d" % h, align_bytes=64) for h in range(halves)]
+        table_scales = [keep.tile([P, J_CHUNK], U8, name="table_scales%d" % h, align_bytes=64) for h in range(halves)]
+
+        def scale_table(h):
             nc.vector.tensor_tensor(
-                grouped[:].rearrange("p (c i) t -> p c t i", i=4),
-                g0[:].rearrange("p t (c i) -> p c t i", i=4),
-                row_factor[:].unsqueeze(1).unsqueeze(3).broadcast_to([P, J_CHUNK // 4, PACK, 4]),
-                ALU.mult,
+                table_grouped[h][:].rearrange("p (c i) t -> p c t i", i=4),
+                lo[:, :, h * J_CHUNK : (h + 1) * J_CHUNK].rearrange("p t (c i) -> p c t i", i=4),
+                mid[:, :, h * J_CHUNK : (h + 1) * J_CHUNK].rearrange("p t (c i) -> p c t i", i=4),
+                ALU.max,
             )
-            codes = keep.tile([P, J_CHUNK], U32, name="table_codes%d" % h, align_bytes=64)
-            scales = keep.tile([P, J_CHUNK], U8, name="table_scales%d" % h, align_bytes=64)
-            nc.vector.quantize_mx(
-                out=codes[:].bitcast(FP8X4), scales=scales[:], in_=grouped[:].rearrange("p j t -> p (j t)")
-            )
-            return codes, scales
 
-        def turn_values():
-            grouped = keep.tile([P, E, PACK], BF16, name="val_grouped", tag="grouped1", align_bytes=64)
-            grouped_words = grouped[:].rearrange("p e t -> p (e t)").bitcast(F32).rearrange("p (k e u) -> p k e u", k=E // P, u=2)
-            for k0 in range(0, E // P, 2):
-                turned = turn_pool.tile([P, 2, 2, P], F32, name="turned")
-                for k in range(k0, k0 + 2):
-                    vp = keep.tile([P, I], BF16, name="val_picked%d" % k)
-                    nc.scalar.activation(vp[:], val_pool[k][:].indirect(token_list[:]), COPY)
-                    words = vp[:].bitcast(F32)
-                    for u in range(2):
-                        nc.tensor.transpose(turned[:, k - k0, u, :], words[:, u : I // 2 : 2], ident[:])
-                nc.scalar.copy(out=grouped_words[:, k0 : k0 + 2, :, :], in_=turned[:].rearrange("p k u e -> p k e u"))
-            codes = keep.tile([P, E], U32, name="val_codes", align_bytes=64)
-            scales = keep.tile([P, E], U8, name="val_scales", align_bytes=64)
-            return grouped, codes, scales
+        def quantise_table(h):
+            nc.vector.quantize_mx(
+                out=table_codes[h][:].bitcast(FP8X4), scales=table_scales[h][:], in_=table_grouped[h][:].rearrange("p j t -> p (j t)")
+            )
+
+        pairs = E // (2 * P)
+        val_grouped = [keep.tile([P, 2 * P, PACK], BF16, name="val_grouped%d" % g, tag=("val_pool2", "val_grouped1")[g], align_bytes=64) for g in range(pairs)]
+        val_codes = [late.tile([P, 2 * P], U32, name="val_codes%d" % g, offset=(4096, 0)[g], align_bytes=64) for g in range(pairs)]
+        val_scales = [keep.tile([P, 2 * P], U8, name="val_scales%d" % g, align_bytes=64) for g in range(pairs)]
+
+        turned = [turn_pool.tile([P, 2, 2, P], F32, name="turned%d" % g, tag="turn%d" % g) for g in range(pairs)]
+
+        def turn_values(k):
+            vp = keep.tile([P, I], BF16, name="val_picked%d" % k)
+            nc.scalar.activation(vp[:], val_pool[k][:].indirect(token_list[:]), COPY)
+            words = vp[:].bitcast(F32)
+            for u in range(2):
+                nc.tensor.transpose(turned[k // 2][:, k % 2, u, :], words[:, u : I // 2 : 2], ident[:])
+
+        def group_values(g):
+            grouped_words = val_grouped[g][:].rearrange("p e t -> p (e t)").bitcast(F32).rearrange("p (k e u) -> p k e u", k=2, u=2)
+            nc.scalar.copy(out=grouped_words, in_=turned[g][:].rearrange("p k u e -> p k e u"))
+
+        def quantise_values(g):
+            nc.vector.quantize_mx(
+                out=val_codes[g][:].bitcast(FP8X4), scales=val_scales[g][:], in_=val_grouped[g][:].rearrange("p e t -> p (e t)")
+            )
 
         out_rows = out.rearrange("(k p) j -> p k j", p=P)
 
-        def second_product(h, val_codes, val_scales, codes, scales, engines):
-            for k0 in range(0, E // P, 2):
-                acc = acc_pool.tile([P, BANK], F32, name="acc")
-                for k in range(k0, k0 + 2):
-                    nc.tensor.matmul_mx(
-                        out=acc[:, (k - k0) * J_CHUNK : (k - k0 + 1) * J_CHUNK],
-                        lhsT=val_codes[:, k * P : (k + 1) * P].bitcast(FP8X4),
-                        lhsT_scale=val_scales[:, k * P : (k + 1) * P],
-                        rhs=codes[:].bitcast(FP8X4),
-                        rhs_scale=scales[:],
-                        start=True,
-                        stop=True,
-                    )
-                res = keep.tile([P, 2, J_CHUNK], F32, name="res%d_%d" % (h, k0))
-                if engines[k0 // 2]:
-                    nc.vector.tensor_copy(out=res[:].rearrange("p k j -> p (k j)"), in_=acc[:])
-                else:
-                    nc.scalar.copy(out=res[:].rearrange("p k j -> p (k j)"), in_=acc[:])
-                nc.sync.dma_start(out=out_rows[:, k0 : k0 + 2, h * J_CHUNK : (h + 1) * J_CHUNK], in_=res[:])
+        def second_product(g, h, ks, on_vector, bank):
+            for n, k in enumerate(ks):
+                nc.tensor.matmul_mx(
+                    out=bank[:, n * J_CHUNK : (n + 1) * J_CHUNK],
+                    lhsT=val_codes[g][:, k * P : (k + 1) * P].bitcast(FP8X4),
+                    lhsT_scale=val_scales[g][:, k * P : (k + 1) * P],
+                    rhs=table_codes[h][:].bitcast(FP8X4),
+                    rhs_scale=table_scales[h][:],
+                    start=True,
+                    stop=True,
+                )
+            res = keep.tile([P, len(ks), J_CHUNK], F32, name="res%d_%d_%d" % (g, h, ks[0]))
+            if on_vector:
+                nc.vector.tensor_copy(out=res[:].rearrange("p k j -> p (k j)"), in_=bank[:, : len(ks) * J_CHUNK])
+            else:
+                nc.scalar.copy(out=res[:].rearrange("p k j -> p (k j)"), in_=bank[:, : len(ks) * J_CHUNK])
+            k0 = 2 * g + ks[0]
+            nc.sync.dma_start(out=out_rows[:, k0 : k0 + len(ks), h * J_CHUNK : (h + 1) * J_CHUNK], in_=res[:])
 
         for t in range(PACK):
-            look_up(0, t, (0, 1) if t < 2 else (0,))
-        g0_first = middle(0, (0, 2))
-        for t in range(PACK):
-            look_up(1, t, (0,) if t < 3 else ())
-        table0 = scale_and_quantise(0, g0_first)
-        val_grouped, val_codes, val_scales = turn_values()
-        g0_second = middle(1, (0, 2))
-        nc.vector.quantize_mx(
-            out=val_codes[:].bitcast(FP8X4), scales=val_scales[:], in_=val_grouped[:].rearrange("p e t -> p (e t)")
-        )
-        second_product(0, val_codes, val_scales, table0[0], table0[1], (False, False))
-        table1 = scale_and_quantise(1, g0_second)
-        second_product(1, val_codes, val_scales, table1[0], table1[1], (True, False))
+            look_up_scalar(t)
+        for t in range(3):
+            look_up_vector(t)
+        upper(0)
+        lower_and_cap(0)
+        upper(1)
+        lower_and_cap(1)
+        look_up_vector(3)
+        nc.vector.tensor_copy(c[:, 3, :], g1[3][:].indirect(column_lists[2][:]))
+        upper(2)
+        lower_and_cap(2)
+        upper(3)
+        lower_and_cap(3)
+        turn_values(0)
+        turn_values(1)
+        turn_values(2)
+        group_values(0)
+        turn_values(3)
+        group_values(1)
+        scale_table(0)
+        quantise_values(0)
+        quantise_table(0)
+        scale_table(1)
+        quantise_table(1)
+        quantise_values(1)
+        second_product(0, 0, (0, 1), False, turn_pool.tile([P, BANK], F32, name="out_bank", tag="turn1"))
+        second_product(0, 1, (0, 1), True, acc_pool.tile([P, BANK], F32, name="acc"))
+        second_product(1, 0, (0, 1), False, acc_pool.tile([P, BANK], F32, name="acc"))
+        second_product(1, 1, (0,), True, acc_pool.tile([P, BANK], F32, name="acc"))
+        second_product(1, 1, (1,), False, acc_pool.tile([P, BANK], F32, name="acc"))

@@ -21,6 +21,7 @@ PACK = 4
 NOTE_CHUNK = 256
 J_CHUNK = 256
 BANK = 512
+SPLIT = 384
 
 
 def tile_attend_tab_middleof3_exchange_kernel(tc, keys_words, keys_scales, notes, rowf, vals, offs, offs2, offs3, offs4, out):
@@ -31,12 +32,6 @@ def tile_attend_tab_middleof3_exchange_kernel(tc, keys_words, keys_scales, notes
         acc_pool = ctx.enter_context(tc.psum_pool(name="acc", bufs=6))
         turn_pool = ctx.enter_context(tc.psum_pool(name="turn", bufs=1))
 
-        token_list = keep.tile([P, I // 16], U16, name="token_list")
-        nc.sync.dma_start(token_list[:], offs)
-        row_factor = keep.tile([P, PACK], F32, name="row_factor")
-        nc.sync.dma_start(out=row_factor[:], in_=rowf.rearrange("(p t) o -> p (t o)", t=PACK))
-        row_spread = keep.tile([P, PACK, J], F32, name="row_spread")
-        nc.scalar.copy(out=row_spread[:], in_=row_factor[:].unsqueeze(2).broadcast_to([P, PACK, J]))
 
         key_scale_pool = keep.tile([P, T], U8, name="key_scale_pool", align_bytes=64)
         nc.vector.memset(key_scale_pool[:].bitcast(I32), 0)
@@ -47,6 +42,8 @@ def tile_attend_tab_middleof3_exchange_kernel(tc, keys_words, keys_scales, notes
             nc.sync.dma_start(out=note_raw[c][:], in_=note_rows[:, :, c * NOTE_CHUNK : (c + 1) * NOTE_CHUNK])
 
         load_notes(0)
+        token_list = keep.tile([P, I // 16], U16, name="token_list")
+        nc.sync.dma_start(token_list[:], offs)
         for q in range(4):
             nc.sync.dma_start(
                 out=key_scale_pool[32 * q : 32 * q + 4, :].bitcast(I32),
@@ -54,6 +51,10 @@ def tile_attend_tab_middleof3_exchange_kernel(tc, keys_words, keys_scales, notes
             )
         key_word_pool = keep.tile([P, T], I32, name="key_word_pool", align_bytes=64)
         nc.sync.dma_start(out=key_word_pool[:], in_=keys_words[0].rearrange("p n t -> p (n t)").bitcast(I32))
+        row_factor = keep.tile([P, PACK], F32, name="row_factor")
+        nc.sync.dma_start(out=row_factor[:], in_=rowf.rearrange("(p t) o -> p (t o)", t=PACK))
+        row_spread = keep.tile([P, PACK, J], F32, name="row_spread")
+        nc.scalar.copy(out=row_spread[:], in_=row_factor[:].unsqueeze(2).broadcast_to([P, PACK, J]))
         for c in range(1, U // NOTE_CHUNK):
             load_notes(c)
 
@@ -73,8 +74,10 @@ def tile_attend_tab_middleof3_exchange_kernel(tc, keys_words, keys_scales, notes
         make_identity(nc, ident[:])
 
         key_scales = keep.tile([P, I], U8, name="key_scales", align_bytes=64)
+        listed_scales = keep.tile([P, I], U8, name="listed_scales", align_bytes=64)
+        nc.vector.tensor_copy(listed_scales[:], key_scale_pool[:].indirect(token_list[:]))
         nc.vector.tensor_copy(
-            key_scales[:].rearrange("p (t s) -> p s t", t=PACK), key_scale_pool[:].indirect(token_list[:])
+            key_scales[:].rearrange("p (t s) -> p t s", t=PACK), listed_scales[:].rearrange("p (s t) -> p t s", t=PACK)
         )
         key_words = keep.tile([P, I], U32, name="key_words", align_bytes=64)
         nc.vector.tensor_copy(
@@ -105,7 +108,7 @@ def tile_attend_tab_middleof3_exchange_kernel(tc, keys_words, keys_scales, notes
                     start=True,
                     stop=True,
                 )
-                if (c, t) in ((2, 3), (3, 0), (3, 1)):
+                if (c, t) in ((2, 3), (3, 0)):
                     nc.vector.tensor_copy(out=g1[t][:, c * NOTE_CHUNK : (c + 1) * NOTE_CHUNK], in_=acc[:, :NOTE_CHUNK])
                 else:
                     nc.scalar.copy(out=g1[t][:, c * NOTE_CHUNK : (c + 1) * NOTE_CHUNK], in_=acc[:, :NOTE_CHUNK])
@@ -117,8 +120,10 @@ def tile_attend_tab_middleof3_exchange_kernel(tc, keys_words, keys_scales, notes
             nc.vector.tensor_tensor(a[:, t, :], g1[t][:].indirect(column_lists[0][:]), row_spread[:, t, :], ALU.mult)
 
         def look_up_scalar(t):
-            nc.scalar.activation(b[:, t, :], g1[t][:].indirect(column_lists[1][:]), COPY)
-            if t < PACK - 1:
+            if t == PACK - 1:
+                nc.scalar.activation(b[:, t, :SPLIT], g1[t][:].indirect(column_lists[1][:, : SPLIT // 16]), COPY)
+            else:
+                nc.scalar.activation(b[:, t, :], g1[t][:].indirect(column_lists[1][:]), COPY)
                 nc.scalar.activation(c[:, t, :], g1[t][:].indirect(column_lists[2][:]), COPY)
 
         def upper(t):
@@ -130,7 +135,7 @@ def tile_attend_tab_middleof3_exchange_kernel(tc, keys_words, keys_scales, notes
 
         halves = J // J_CHUNK
         table_grouped = [late.tile([P, J_CHUNK, PACK], BF16, name="table_grouped%d" % h, offset=1024 * h, align_bytes=64) for h in range(halves)]
-        table_codes = [keep.tile([P, J_CHUNK], U32, name="table_codes%d" % h, align_bytes=64) for h in range(halves)]
+        table_codes = [keep.tile([P, J_CHUNK], U32, name="table_codes%d" % h, tag=("table_codes0", "val_grouped1")[h], align_bytes=64) for h in range(halves)]
         table_scales = [keep.tile([P, J_CHUNK], U8, name="table_scales%d" % h, align_bytes=64) for h in range(halves)]
 
         def scale_table(h):
@@ -200,6 +205,7 @@ def tile_attend_tab_middleof3_exchange_kernel(tc, keys_words, keys_scales, notes
         lower_and_cap(1)
         look_up_vector(3)
         nc.vector.tensor_copy(c[:, 3, :], g1[3][:].indirect(column_lists[2][:]))
+        nc.vector.tensor_copy(b[:, 3, SPLIT:], g1[3][:].indirect(column_lists[1][:, SPLIT // 16 :]))
         upper(2)
         lower_and_cap(2)
         upper(3)
@@ -214,10 +220,10 @@ def tile_attend_tab_middleof3_exchange_kernel(tc, keys_words, keys_scales, notes
         quantise_values(0)
         quantise_table(0)
         scale_table(1)
-        quantise_table(1)
         quantise_values(1)
+        quantise_table(1)
         second_product(0, 0, (0, 1), False, turn_pool.tile([P, BANK], F32, name="out_bank", tag="turn1"))
-        second_product(0, 1, (0, 1), True, acc_pool.tile([P, BANK], F32, name="acc"))
         second_product(1, 0, (0, 1), False, acc_pool.tile([P, BANK], F32, name="acc"))
-        second_product(1, 1, (0,), True, acc_pool.tile([P, BANK], F32, name="acc"))
-        second_product(1, 1, (1,), False, acc_pool.tile([P, BANK], F32, name="acc"))
+        for g in range(pairs):
+            second_product(g, 1, (0,), True, acc_pool.tile([P, BANK], F32, name="acc"))
+            second_product(g, 1, (1,), False, acc_pool.tile([P, BANK], F32, name="acc"))

from contextlib import ExitStack

import concourse.mybir as mybir
from concourse.masks import make_identity

D, T, I, J, U, E = 512, 2048, 512, 512, 1024, 512
FLOPS = 2 * D * I * U + 2 * I * E * J

F32 = mybir.dt.float32
BF16 = mybir.dt.bfloat16
I32 = mybir.dt.int32
U32 = mybir.dt.uint32
U16 = mybir.dt.uint16
U8 = mybir.dt.uint8
FP8X4 = mybir.dt.float8_e4m3fn_x4
ALU = mybir.AluOpType
COPY = mybir.ActivationFunctionType.Copy

P = 128
PACK = 4
NOTE_CHUNK = 256
J_CHUNK = 256
BANK = 512
SPLIT = 384


def tile_attend_tab_middleof3_exchange_kernel(tc, keys_words, keys_scales, notes, rowf, vals, offs, offs2, offs3, offs4, out):
    nc = tc.nc
    with ExitStack() as ctx:
        keep = ctx.enter_context(tc.tile_pool(name="keep", bufs=1))
        late = ctx.enter_context(tc.tile_pool(name="late", bufs=1))
        acc_pool = ctx.enter_context(tc.psum_pool(name="acc", bufs=6))
        turn_pool = ctx.enter_context(tc.psum_pool(name="turn", bufs=1))


        key_scale_pool = keep.tile([P, T], U8, name="key_scale_pool", align_bytes=64)
        nc.vector.memset(key_scale_pool[:].bitcast(I32), 0)
        note_rows = notes.rearrange("(p t) u -> p t u", t=PACK)
        note_raw = [keep.tile([P, PACK, NOTE_CHUNK], F32, name="note_raw%d" % c) for c in range(U // NOTE_CHUNK)]

        def load_notes(c):
            nc.sync.dma_start(out=note_raw[c][:], in_=note_rows[:, :, c * NOTE_CHUNK : (c + 1) * NOTE_CHUNK])

        load_notes(0)
        token_list = keep.tile([P, I // 16], U16, name="token_list")
        nc.sync.dma_start(token_list[:], offs)
        for q in range(4):
            nc.sync.dma_start(
                out=key_scale_pool[32 * q : 32 * q + 4, :].bitcast(I32),
                in_=keys_scales[0, 4 * q : 4 * q + 4, :].bitcast(I32),
            )
        key_word_pool = keep.tile([P, T], I32, name="key_word_pool", align_bytes=64)
        nc.sync.dma_start(out=key_word_pool[:], in_=keys_words[0].rearrange("p n t -> p (n t)").bitcast(I32))
        row_factor = keep.tile([P, PACK], F32, name="row_factor")
        nc.sync.dma_start(out=row_factor[:], in_=rowf.rearrange("(p t) o -> p (t o)", t=PACK))
        row_spread = keep.tile([P, PACK, J], F32, name="row_spread")
        nc.scalar.copy(out=row_spread[:], in_=row_factor[:].unsqueeze(2).broadcast_to([P, PACK, J]))
        for c in range(1, U // NOTE_CHUNK):
            load_notes(c)

        column_lists = []
        for n, src in enumerate((offs2, offs3, offs4)):
            lst = keep.tile([P, J // 16], U16, name="column_list%d" % n)
            nc.sync.dma_start(lst[:], src)
            column_lists.append(lst)

        val_pool = []
        for k in range(E // P):
            vp = keep.tile([P, T], F32, name="val_pool%d" % k, align_bytes=64)
            nc.sync.dma_start(out=vp[:], in_=vals[k * P : (k + 1) * P, :])
            val_pool.append(vp)

        ident = keep.tile([P, P], F32, name="ident")
        make_identity(nc, ident[:])

        key_scales = keep.tile([P, I], U8, name="key_scales", align_bytes=64)
        listed_scales = keep.tile([P, I], U8, name="listed_scales", align_bytes=64)
        nc.vector.tensor_copy(listed_scales[:], key_scale_pool[:].indirect(token_list[:]))
        nc.vector.tensor_copy(
            key_scales[:].rearrange("p (t s) -> p t s", t=PACK), listed_scales[:].rearrange("p (s t) -> p t s", t=PACK)
        )
        key_words = keep.tile([P, I], U32, name="key_words", align_bytes=64)
        nc.vector.tensor_copy(
            key_words[:].rearrange("p (t s) -> p s t", t=PACK),
            key_word_pool[:].bitcast(U32).indirect(token_list[:]),
        )

        g1 = [keep.tile([P, U], F32, name="g1_%d" % t) for t in range(PACK)]
        for c in range(U // NOTE_CHUNK):
            grouped = keep.tile([P, NOTE_CHUNK, PACK], BF16, name="note_grouped%d" % c, align_bytes=64)
            nc.vector.tensor_copy(
                out=grouped[:].rearrange("p (c i) t -> p c t i", i=4),
                in_=note_raw[c][:].rearrange("p t (c i) -> p c t i", i=4),
            )
            codes = keep.tile([P, NOTE_CHUNK], U32, name="note_codes%d" % c, align_bytes=64)
            scales = keep.tile([P, NOTE_CHUNK], U8, name="note_scales%d" % c, align_bytes=64)
            nc.vector.quantize_mx(
                out=codes[:].bitcast(FP8X4), scales=scales[:], in_=grouped[:].rearrange("p u t -> p (u t)")
            )
            for t in range(PACK):
                acc = acc_pool.tile([P, BANK], F32, name="acc")
                nc.tensor.matmul_mx(
                    out=acc[:, :NOTE_CHUNK],
                    lhsT=key_words[:, t * P : (t + 1) * P].bitcast(FP8X4),
                    lhsT_scale=key_scales[:, t * P : (t + 1) * P],
                    rhs=codes[:].bitcast(FP8X4),
                    rhs_scale=scales[:],
                    start=True,
                    stop=True,
                )
                if (c, t) in ((2, 3), (3, 0)):
                    nc.vector.tensor_copy(out=g1[t][:, c * NOTE_CHUNK : (c + 1) * NOTE_CHUNK], in_=acc[:, :NOTE_CHUNK])
                else:
                    nc.scalar.copy(out=g1[t][:, c * NOTE_CHUNK : (c + 1) * NOTE_CHUNK], in_=acc[:, :NOTE_CHUNK])

        a, b, c, lo, mid = (keep.tile([P, PACK, J], F32, name=n) for n in ("a", "b", "c", "lo", "mid"))
        hi = late.tile([P, PACK, J], F32, name="hi", offset=4096, align_bytes=64)

        def look_up_vector(t):
            nc.vector.tensor_tensor(a[:, t, :], g1[t][:].indirect(column_lists[0][:]), row_spread[:, t, :], ALU.mult)

        def look_up_scalar(t):
            if t == PACK - 1:
                nc.scalar.activation(b[:, t, :SPLIT], g1[t][:].indirect(column_lists[1][:, : SPLIT // 16]), COPY)
            else:
                nc.scalar.activation(b[:, t, :], g1[t][:].indirect(column_lists[1][:]), COPY)
                nc.scalar.activation(c[:, t, :], g1[t][:].indirect(column_lists[2][:]), COPY)

        def upper(t):
            nc.vector.scalar_tensor_tensor(hi[:, t, :], b[:, t, :], row_factor[:, t : t + 1], a[:, t, :], ALU.mult, ALU.max)

        def lower_and_cap(t):
            nc.vector.scalar_tensor_tensor(lo[:, t, :], b[:, t, :], row_factor[:, t : t + 1], a[:, t, :], ALU.mult, ALU.min)
            nc.vector.scalar_tensor_tensor(mid[:, t, :], c[:, t, :], row_factor[:, t : t + 1], hi[:, t, :], ALU.mult, ALU.min)

        halves = J // J_CHUNK
        table_grouped = [late.tile([P, J_CHUNK, PACK], BF16, name="table_grouped%d" % h, offset=1024 * h, align_bytes=64) for h in range(halves)]
        table_codes = [keep.tile([P, J_CHUNK], U32, name="table_codes%d" % h, tag=("table_codes0", "val_grouped1")[h], align_bytes=64) for h in range(halves)]
        table_scales = [keep.tile([P, J_CHUNK], U8, name="table_scales%d" % h, align_bytes=64) for h in range(halves)]

        def scale_table(h):
            nc.vector.tensor_tensor(
                table_grouped[h][:].rearrange("p (c i) t -> p c t i", i=4),
                lo[:, :, h * J_CHUNK : (h + 1) * J_CHUNK].rearrange("p t (c i) -> p c t i", i=4),
                mid[:, :, h * J_CHUNK : (h + 1) * J_CHUNK].rearrange("p t (c i) -> p c t i", i=4),
                ALU.max,
            )

        def quantise_table(h):
            nc.vector.quantize_mx(
                out=table_codes[h][:].bitcast(FP8X4), scales=table_scales[h][:], in_=table_grouped[h][:].rearrange("p j t -> p (j t)")
            )

        pairs = E // (2 * P)
        val_grouped = [keep.tile([P, 2 * P, PACK], BF16, name="val_grouped%d" % g, tag=("val_pool2", "val_grouped1")[g], align_bytes=64) for g in range(pairs)]
        val_codes = [late.tile([P, 2 * P], U32, name="val_codes%d" % g, offset=(4096, 0)[g], align_bytes=64) for g in range(pairs)]
        val_scales = [keep.tile([P, 2 * P], U8, name="val_scales%d" % g, align_bytes=64) for g in range(pairs)]

        turned = [turn_pool.tile([P, 2, 2, P], F32, name="turned%d" % g, tag="turn%d" % g) for g in range(pairs)]

        def turn_values(k):
            vp = keep.tile([P, I], BF16, name="val_picked%d" % k)
            nc.scalar.activation(vp[:], val_pool[k][:].indirect(token_list[:]), COPY)
            words = vp[:].bitcast(F32)
            for u in range(2):
                nc.tensor.transpose(turned[k // 2][:, k % 2, u, :], words[:, u : I // 2 : 2], ident[:])

        def group_values(g):
            grouped_words = val_grouped[g][:].rearrange("p e t -> p (e t)").bitcast(F32).rearrange("p (k e u) -> p k e u", k=2, u=2)
            nc.scalar.copy(out=grouped_words, in_=turned[g][:].rearrange("p k u e -> p k e u"))

        def quantise_values(g):
            nc.vector.quantize_mx(
                out=val_codes[g][:].bitcast(FP8X4), scales=val_scales[g][:], in_=val_grouped[g][:].rearrange("p e t -> p (e t)")
            )

        out_rows = out.rearrange("(k p) j -> p k j", p=P)

        def second_product(g, h, ks, on_vector, bank):
            for n, k in enumerate(ks):
                nc.tensor.matmul_mx(
                    out=bank[:, n * J_CHUNK : (n + 1) * J_CHUNK],
                    lhsT=val_codes[g][:, k * P : (k + 1) * P].bitcast(FP8X4),
                    lhsT_scale=val_scales[g][:, k * P : (k + 1) * P],
                    rhs=table_codes[h][:].bitcast(FP8X4),
                    rhs_scale=table_scales[h][:],
                    start=True,
                    stop=True,
                )
            res = keep.tile([P, len(ks), J_CHUNK], F32, name="res%d_%d_%d" % (g, h, ks[0]))
            if on_vector:
                nc.vector.tensor_copy(out=res[:].rearrange("p k j -> p (k j)"), in_=bank[:, : len(ks) * J_CHUNK])
            else:
                nc.scalar.copy(out=res[:].rearrange("p k j -> p (k j)"), in_=bank[:, : len(ks) * J_CHUNK])
            k0 = 2 * g + ks[0]
            nc.sync.dma_start(out=out_rows[:, k0 : k0 + len(ks), h * J_CHUNK : (h + 1) * J_CHUNK], in_=res[:])

        for t in range(PACK):
            look_up_scalar(t)
        for t in range(3):
            look_up_vector(t)
        upper(0)
        lower_and_cap(0)
        upper(1)
        lower_and_cap(1)
        look_up_vector(3)
        nc.vector.tensor_copy(c[:, 3, :], g1[3][:].indirect(column_lists[2][:]))
        nc.vector.tensor_copy(b[:, 3, SPLIT:], g1[3][:].indirect(column_lists[1][:, SPLIT // 16 :]))
        upper(2)
        lower_and_cap(2)
        upper(3)
        lower_and_cap(3)
        turn_values(0)
        turn_values(1)
        turn_values(2)
        group_values(0)
        turn_values(3)
        group_values(1)
        scale_table(0)
        quantise_values(0)
        quantise_table(0)
        scale_table(1)
        quantise_values(1)
        quantise_table(1)
        second_product(0, 0, (0, 1), False, turn_pool.tile([P, BANK], F32, name="out_bank", tag="turn1"))
        second_product(1, 0, (0, 1), False, acc_pool.tile([P, BANK], F32, name="acc"))
        for g in range(pairs):
            second_product(g, 1, (0,), True, acc_pool.tile([P, BANK], F32, name="acc"))
            second_product(g, 1, (1,), False, acc_pool.tile([P, BANK], F32, name="acc"))
